import numpy as np
import ml_dtypes


def mxq(x, axis, fmt="e4m3"):
    dtype, down = {"e4m3": (ml_dtypes.float8_e4m3fn, 7), "e5m2": (ml_dtypes.float8_e5m2, 14)}[fmt]
    v = np.moveaxis(np.asarray(x, np.float32).astype(ml_dtypes.bfloat16).astype(np.float64), axis, -1)
    blocks = v.reshape(v.shape[:-1] + (-1, 32))
    amax = np.abs(blocks).max(-1, keepdims=True)
    byte = np.maximum(np.where(amax > 0, np.frexp(amax)[1] - 1 + 127, 0) - down, 1)
    scale = np.exp2(byte - 127.0)
    codes = (blocks / scale).astype(np.float32).astype(dtype).astype(np.float64)
    return np.moveaxis((codes * scale).reshape(v.shape), -1, axis)


WIDE = False


def mx_kscale(k, group=512):
    if not WIDE:
        return np.ones(k)
    levels = np.array([18, -18])
    if group != 512:
        return np.exp2(np.random.permutation(np.resize(levels, k // group))).repeat(group)
    if k % 512:
        return np.exp2(np.random.permutation(np.resize(levels, k // 32))).repeat(32)
    a = np.empty((k // 512, 16))
    for p in range(k // 512):
        a[p, :8] = np.random.permutation(np.resize(levels, 8))
        for g in range(8):
            far = levels[np.abs(levels - a[p, g]) >= 10]
            a[p, g + 8] = far[np.random.randint(len(far))]
    return np.exp2(a.ravel()).repeat(32)


def f64(x):
    return np.asarray(x).astype(np.float64)


def sigmoid(v):
    return 1.0 / (1.0 + np.exp(-v))


G, D, M, N, L = 4, 128, 128, 512, 640


def setup_inputs():
    n = np.random.standard_normal
    s_d = mx_kscale(D, 0)
    return {
        "x": (n((G, D, L)) * s_d[:, None]).astype(np.float32),
        "w0": (n((G, D, M)) / np.sqrt(2 * D) / s_d[:, None]).astype(np.float32),
        "w1": (n((G, D, M)) / np.sqrt(2 * D) / s_d[:, None]).astype(np.float32),
        "u0": (n((G, D, M)) / np.sqrt(2 * D) / s_d[:, None]).astype(np.float32),
        "u1": (n((G, D, M)) / np.sqrt(2 * D) / s_d[:, None]).astype(np.float32),
    }


def reference(x, w0, w1, u0, u1):
    w0q = mxq(f64(w0), 1, "e4m3")
    xq = mxq(f64(x), 1, "e4m3")
    w1q = mxq(f64(w1), 1, "e4m3")
    z = (w0q.transpose(0, 2, 1) @ xq[..., :512]) + (w1q.transpose(0, 2, 1) @ xq[..., 128 : 640])
    u0q = mxq(f64(u0), 1, "e4m3")
    u1q = mxq(f64(u1), 1, "e4m3")
    g_ = (u0q.transpose(0, 2, 1) @ xq[..., :512]) + (u1q.transpose(0, 2, 1) @ xq[..., 128 : 640])
    y = np.tanh(z) * sigmoid(g_)
    return y

@@ -1,0 +1,134 @@
+from contextlib import ExitStack
+
+import concourse.mybir as mybir
+
+G, D, M, N, L = 4, 128, 128, 512, 640
+FLOPS = 2 * 4 * G * D * M * N
+
+F32 = mybir.dt.float32
+BF16 = mybir.dt.bfloat16
+U32 = mybir.dt.uint32
+U8 = mybir.dt.uint8
+FP8X4 = mybir.dt.float8_e4m3fn_x4
+ACT = mybir.ActivationFunctionType
+ALU = mybir.AluOpType
+
+P = 128
+PACK = 4
+ROWS = D // PACK
+C = 128
+RUN = 4
+
+
+def tile_rows_conv_wave_kernel(tc, x, w0, w1, u0, u1, out):
+    nc = tc.nc
+    src = {"w0": w0, "w1": w1, "u0": u0, "u1": u1}
+    for c in range(L // C):
+        src["x%d" % c] = x[:, :, c * C : (c + 1) * C]
+    order = ["w0", "w1", "x0", "x1", "x2", "u0", "u1", "x3", "x4"]
+    place = {name: i for i, name in enumerate(order)}
+
+    with ExitStack() as ctx:
+        sb = ctx.enter_context(tc.tile_pool(name="sb", bufs=1))
+        ps = ctx.enter_context(tc.psum_pool(name="ps", bufs=1))
+        ctx.enter_context(tc.manual_schedule())
+
+        raw = sb.tile([P, len(order), PACK, C], F32, name="raw", align_bytes=64)
+        grouped = sb.tile([P, len(order), C * PACK], BF16, name="grouped", align_bytes=64)
+        codes = sb.tile([P, len(order), C], U32, name="codes", align_bytes=64)
+        scales = sb.tile([P, len(order), C], U8, name="scales", align_bytes=64)
+        th = sb.tile([P, G, N], F32, name="th", align_bytes=64)
+        sg = sb.tile([P, G, N], F32, name="sg", align_bytes=64)
+        y = sb.tile([P, G, N], F32, name="y", align_bytes=64)
+        warm_in = sb.tile([P, 8], F32, name="warm_in")
+        warm_out = sb.tile([P, 8], F32, name="warm_out")
+        bank_a = [ps.tile([P, 512], F32, name="bank_a%d" % g) for g in range(G)]
+        bank_b = [ps.tile([P, 512], F32, name="bank_b%d" % g) for g in range(G)]
+
+        def interleave(engine_copy, name):
+            i = place[name]
+            engine_copy(
+                out=grouped[:, i, :].rearrange("p (c r j) -> p c j r", r=RUN, j=PACK),
+                in_=raw[:, i, :, :].rearrange("p j (c r) -> p c j r", r=RUN),
+            )
+
+        def quantize(name, count=1):
+            i = place[name]
+            nc.vector.quantize_mx(
+                out=codes[:, i : i + count, :].rearrange("p a c -> p (a c)").bitcast(FP8X4),
+                scales=scales[:, i : i + count, :].rearrange("p a c -> p (a c)"),
+                in_=grouped[:, i : i + count, :].rearrange("p a c -> p (a c)"),
+            )
+
+        def tap(banks, col, wname, xname, first):
+            for g in range(G):
+                rows = slice(g * ROWS, (g + 1) * ROWS)
+                nc.tensor.matmul_mx(
+                    out=banks[g][:, col : col + C],
+                    lhsT=codes[rows, place[wname], :].bitcast(FP8X4),
+                    lhsT_scale=scales[rows, place[wname], :],
+                    rhs=codes[rows, place[xname], :].bitcast(FP8X4),
+                    rhs_scale=scales[rows, place[xname], :],
+                    start=first,
+                    stop=not first,
+                )
+
+        def conv(banks, col, kind, c):
+            tap(banks, col, kind + "0", "x%d" % c, True)
+            tap(banks, col, kind + "1", "x%d" % (c + 1), False)
+
+        def act(func, dst, banks, col, g, n0, width):
+            nc.scalar.activation(out=dst[:, g, n0 : n0 + width], in_=banks[g][:, col : col + width], func=func)
+
+        def finish(g, n0, width):
+            cols = slice(n0, n0 + width)
+            nc.vector.tensor_tensor(out=y[:, g, cols], in0=th[:, g, cols], in1=sg[:, g, cols], op=ALU.mult)
+            nc.sync.dma_start(out=out[g, :, cols], in_=y[:, g, cols])
+
+        for name in order:
+            nc.sync.dma_start(out=raw[:, place[name], :, :], in_=src[name].rearrange("g (p j) c -> (g p) j c", j=PACK))
+
+        nc.vector.memset(warm_in[:], 0.0)
+        nc.scalar.activation(out=warm_out[:], in_=warm_in[:], func=ACT.Sigmoid)
+
+        interleave(nc.scalar.copy, "w0")
+        interleave(nc.scalar.copy, "w1")
+        vcopy = nc.vector.tensor_copy
+        quantize("w0")
+        interleave(vcopy, "x0")
+        quantize("w1")
+        quantize("x0")
+        interleave(vcopy, "x1")
+        quantize("x1")
+        conv(bank_a, 0, "w", 0)
+        for g in range(G):
+            act(ACT.Tanh, th, bank_a, 0, g, 0, C)
+        interleave(vcopy, "x2")
+        quantize("x2")
+        conv(bank_b, 0, "w", 1)
+        for g in range(G):
+            act(ACT.Tanh, th, bank_b, 0, g, C, C)
+        interleave(vcopy, "u0")
+        quantize("u0")
+        interleave(vcopy, "u1")
+        quantize("u1")
+        conv(bank_a, C, "u", 0)
+        conv(bank_a, 2 * C, "u", 1)
+        for g in range(G):
+            act(ACT.Sigmoid, sg, bank_a, C, g, 0, 2 * C)
+        interleave(vcopy, "x3")
+        quantize("x3")
+        conv(bank_b, C, "w", 2)
+        interleave(vcopy, "x4")
+        quantize("x4")
+        conv(bank_b, 2 * C, "w", 3)
+        conv(bank_a, C, "u", 2)
+        conv(bank_a, 2 * C, "u", 3)
+        for g in range(G):
+            finish(g, 0, 2 * C)
+        act(ACT.Tanh, th, bank_b, C, 0, 2 * C, 2 * C)
+        for g in range(G):
+            if g + 1 < G:
+                act(ACT.Tanh, th, bank_b, C, g + 1, 2 * C, 2 * C)
+            act(ACT.Sigmoid, sg, bank_a, C, g, 2 * C, 2 * C)
+            finish(g, 2 * C, 2 * C)

@@ -16,119 +16,144 @@ ALU = mybir.AluOpType
 P = 128
 PACK = 4
 ROWS = D // PACK
-C = 128
+DIL = 128
+HALF = N // 2
 RUN = 4
+W0, W1, U0, U1 = range(4)
 
 
 def tile_rows_conv_wave_kernel(tc, x, w0, w1, u0, u1, out):
     nc = tc.nc
-    src = {"w0": w0, "w1": w1, "u0": u0, "u1": u1}
-    for c in range(L // C):
-        src["x%d" % c] = x[:, :, c * C : (c + 1) * C]
-    order = ["w0", "w1", "x0", "x1", "x2", "u0", "u1", "x3", "x4"]
-    place = {name: i for i, name in enumerate(order)}
 
     with ExitStack() as ctx:
         sb = ctx.enter_context(tc.tile_pool(name="sb", bufs=1))
         ps = ctx.enter_context(tc.psum_pool(name="ps", bufs=1))
         ctx.enter_context(tc.manual_schedule())
 
-        raw = sb.tile([P, len(order), PACK, C], F32, name="raw", align_bytes=64)
-        grouped = sb.tile([P, len(order), C * PACK], BF16, name="grouped", align_bytes=64)
-        codes = sb.tile([P, len(order), C], U32, name="codes", align_bytes=64)
-        scales = sb.tile([P, len(order), C], U8, name="scales", align_bytes=64)
+        w_raw = sb.tile([P, 4, PACK, M], F32, name="w_raw", align_bytes=64)
+        w_bf = sb.tile([P, 4, M * PACK], BF16, name="w_bf", align_bytes=64)
+        w_codes = sb.tile([P, 4, M], U32, name="w_codes", align_bytes=64)
+        w_scales = sb.tile([P, 4, M], U8, name="w_scales", align_bytes=64)
+        x_raw = sb.tile([P, PACK, L], F32, name="x_raw", align_bytes=64)
+        x_bf = sb.tile([P, L * PACK], BF16, name="x_bf", align_bytes=64)
+        x_codes = sb.tile([P, HALF + L], U32, name="x_codes", align_bytes=64)
+        x_scales = sb.tile([P, HALF + L], U8, name="x_scales", align_bytes=64)
         th = sb.tile([P, G, N], F32, name="th", align_bytes=64)
         sg = sb.tile([P, G, N], F32, name="sg", align_bytes=64)
         y = sb.tile([P, G, N], F32, name="y", align_bytes=64)
         warm_in = sb.tile([P, 8], F32, name="warm_in")
         warm_out = sb.tile([P, 8], F32, name="warm_out")
-        bank_a = [ps.tile([P, 512], F32, name="bank_a%d" % g) for g in range(G)]
-        bank_b = [ps.tile([P, 512], F32, name="bank_b%d" % g) for g in range(G)]
+        z_bank = [ps.tile([P, N], F32, name="z_bank%d" % g) for g in range(G)]
+        g_bank = [ps.tile([P, N], F32, name="g_bank%d" % g) for g in range(G)]
 
-        def interleave(engine_copy, name):
-            i = place[name]
+        x_rows = x.rearrange("g (p j) l -> (g p) j l", j=PACK)
+
+        def load_x(l0, l1):
+            nc.sync.dma_start(out=x_raw[:, :, l0:l1], in_=x_rows[:, :, l0:l1])
+
+        def load_w(i, w):
+            nc.sync.dma_start(out=w_raw[:, i, :, :], in_=w.rearrange("g (p j) m -> (g p) j m", j=PACK))
+
+        def interleave(engine_copy, dst, src):
             engine_copy(
-                out=grouped[:, i, :].rearrange("p (c r j) -> p c j r", r=RUN, j=PACK),
-                in_=raw[:, i, :, :].rearrange("p j (c r) -> p c j r", r=RUN),
+                out=dst.rearrange("p (c r j) -> p c j r", r=RUN, j=PACK),
+                in_=src.rearrange("p j (c r) -> p c j r", r=RUN),
             )
 
-        def quantize(name, count=1):
-            i = place[name]
+        def copy_x(l0, l1):
+            interleave(nc.vector.tensor_copy, x_bf[:, PACK * l0 : PACK * l1], x_raw[:, :, l0:l1])
+
+        def copy_w(engine_copy, i):
+            interleave(engine_copy, w_bf[:, i, :], w_raw[:, i, :, :])
+
+        def quantize_x(l0, l1):
             nc.vector.quantize_mx(
-                out=codes[:, i : i + count, :].rearrange("p a c -> p (a c)").bitcast(FP8X4),
-                scales=scales[:, i : i + count, :].rearrange("p a c -> p (a c)"),
-                in_=grouped[:, i : i + count, :].rearrange("p a c -> p (a c)"),
+                out=x_codes[:, HALF + l0 : HALF + l1].bitcast(FP8X4),
+                scales=x_scales[:, HALF + l0 : HALF + l1],
+                in_=x_bf[:, PACK * l0 : PACK * l1],
             )
 
-        def tap(banks, col, wname, xname, first):
+        def quantize_w(i):
+            nc.vector.quantize_mx(out=w_codes[:, i, :].bitcast(FP8X4), scales=w_scales[:, i, :], in_=w_bf[:, i, :])
+
+        def tap(banks, g, i, half, shift):
+            rows = slice(g * ROWS, (g + 1) * ROWS)
+            cols = slice(half * HALF + shift * DIL, half * HALF + shift * DIL + N)
+            nc.tensor.matmul_mx(
+                out=banks[g][:],
+                lhsT=w_codes[rows, i, :].bitcast(FP8X4),
+                lhsT_scale=w_scales[rows, i, :],
+                rhs=x_codes[rows, cols].bitcast(FP8X4),
+                rhs_scale=x_scales[rows, cols],
+                start=(shift == 0),
+                stop=(shift == 1),
+            )
+
+        def taps(banks, i, half, shift):
             for g in range(G):
-                rows = slice(g * ROWS, (g + 1) * ROWS)
-                nc.tensor.matmul_mx(
-                    out=banks[g][:, col : col + C],
-                    lhsT=codes[rows, place[wname], :].bitcast(FP8X4),
-                    lhsT_scale=scales[rows, place[wname], :],
-                    rhs=codes[rows, place[xname], :].bitcast(FP8X4),
-                    rhs_scale=scales[rows, place[xname], :],
-                    start=first,
-                    stop=not first,
-                )
+                tap(banks, g, i, half, shift)
 
-        def conv(banks, col, kind, c):
-            tap(banks, col, kind + "0", "x%d" % c, True)
-            tap(banks, col, kind + "1", "x%d" % (c + 1), False)
+        def act(func, dst, banks, g, half):
+            nc.scalar.activation(out=dst[:, g, half * HALF : (half + 1) * HALF], in_=banks[g][:, HALF:], func=func)
 
-        def act(func, dst, banks, col, g, n0, width):
-            nc.scalar.activation(out=dst[:, g, n0 : n0 + width], in_=banks[g][:, col : col + width], func=func)
-
-        def finish(g, n0, width):
-            cols = slice(n0, n0 + width)
+        def finish(g, half):
+            cols = slice(half * HALF, (half + 1) * HALF)
             nc.vector.tensor_tensor(out=y[:, g, cols], in0=th[:, g, cols], in1=sg[:, g, cols], op=ALU.mult)
             nc.sync.dma_start(out=out[g, :, cols], in_=y[:, g, cols])
 
-        for name in order:
-            nc.sync.dma_start(out=raw[:, place[name], :, :], in_=src[name].rearrange("g (p j) c -> (g p) j c", j=PACK))
+        load_x(0, 256)
+        load_w(W0, w0)
+        load_w(W1, w1)
+        load_x(256, 384)
+        load_w(U0, u0)
+        load_w(U1, u1)
+        load_x(384, 512)
+        load_x(512, 640)
 
-        nc.vector.memset(warm_in[:], 0.0)
+        nc.gpsimd.memset(warm_in[:], 0.0)
+        nc.gpsimd.memset(x_codes[:, :HALF], 0)
+        nc.gpsimd.memset(x_scales[:, :HALF].bitcast(U32), 0)
         nc.scalar.activation(out=warm_out[:], in_=warm_in[:], func=ACT.Sigmoid)
 
-        interleave(nc.scalar.copy, "w0")
-        interleave(nc.scalar.copy, "w1")
-        vcopy = nc.vector.tensor_copy
-        quantize("w0")
-        interleave(vcopy, "x0")
-        quantize("w1")
-        quantize("x0")
-        interleave(vcopy, "x1")
-        quantize("x1")
-        conv(bank_a, 0, "w", 0)
+        copy_x(0, 256)
+        quantize_x(0, 256)
+        copy_w(nc.scalar.copy, W0)
+        quantize_w(W0)
+        taps(z_bank, W0, 0, 0)
+        copy_w(nc.scalar.copy, W1)
+        copy_x(256, 384)
+        quantize_w(W1)
+        quantize_x(256, 384)
+        taps(z_bank, W1, 0, 1)
         for g in range(G):
-            act(ACT.Tanh, th, bank_a, 0, g, 0, C)
-        interleave(vcopy, "x2")
-        quantize("x2")
-        conv(bank_b, 0, "w", 1)
+            act(ACT.Tanh, th, z_bank, g, 0)
+
+        copy_w(nc.vector.tensor_copy, U0)
+        quantize_w(U0)
+        taps(g_bank, U0, 0, 0)
+        copy_w(nc.vector.tensor_copy, U1)
+        quantize_w(U1)
+        taps(g_bank, U1, 0, 1)
         for g in range(G):
-            act(ACT.Tanh, th, bank_b, 0, g, C, C)
-        interleave(vcopy, "u0")
-        quantize("u0")
-        interleave(vcopy, "u1")
-        quantize("u1")
-        conv(bank_a, C, "u", 0)
-        conv(bank_a, 2 * C, "u", 1)
-        for g in range(G):
-            act(ACT.Sigmoid, sg, bank_a, C, g, 0, 2 * C)
-        interleave(vcopy, "x3")
-        quantize("x3")
-        conv(bank_b, C, "w", 2)
-        interleave(vcopy, "x4")
-        quantize("x4")
-        conv(bank_b, 2 * C, "w", 3)
-        conv(bank_a, C, "u", 2)
-        conv(bank_a, 2 * C, "u", 3)
-        for g in range(G):
-            finish(g, 0, 2 * C)
-        act(ACT.Tanh, th, bank_b, C, 0, 2 * C, 2 * C)
+            act(ACT.Sigmoid, sg, g_bank, g, 0)
+
+        copy_x(384, 512)
+        quantize_x(384, 512)
+        taps(z_bank, W0, 1, 0)
+        copy_x(512, 640)
+        quantize_x(512, 640)
+        taps(z_bank, W1, 1, 1)
+        tap(g_bank, 0, U0, 1, 0)
         for g in range(G):
             if g + 1 < G:
-                act(ACT.Tanh, th, bank_b, C, g + 1, 2 * C, 2 * C)
-            act(ACT.Sigmoid, sg, bank_a, C, g, 2 * C, 2 * C)
-            finish(g, 2 * C, 2 * C)
+                tap(g_bank, g + 1, U0, 1, 0)
+            tap(g_bank, g, U1, 1, 1)
+        for g in range(G):
+            finish(g, 0)
+
+        act(ACT.Tanh, th, z_bank, 0, 1)
+        for g in range(G):
+            if g + 1 < G:
+                act(ACT.Tanh, th, z_bank, g + 1, 1)
+            act(ACT.Sigmoid, sg, g_bank, g, 1)
+            finish(g, 1)

@@ -17,7 +17,7 @@ P = 128
 PACK = 4
 ROWS = D // PACK
 DIL = 128
-HALF = N // 2
+PAD = 256
 RUN = 4
 W0, W1, U0, U1 = range(4)
 
@@ -36,15 +36,15 @@ def tile_rows_conv_wave_kernel(tc, x, w0, w1, u0, u1, out):
         w_scales = sb.tile([P, 4, M], U8, name="w_scales", align_bytes=64)
         x_raw = sb.tile([P, PACK, L], F32, name="x_raw", align_bytes=64)
         x_bf = sb.tile([P, L * PACK], BF16, name="x_bf", align_bytes=64)
-        x_codes = sb.tile([P, HALF + L], U32, name="x_codes", align_bytes=64)
-        x_scales = sb.tile([P, HALF + L], U8, name="x_scales", align_bytes=64)
+        x_codes = sb.tile([P, PAD + L], U32, name="x_codes", align_bytes=64)
+        x_scales = sb.tile([P, PAD + L], U8, name="x_scales", align_bytes=64)
         th = sb.tile([P, G, N], F32, name="th", align_bytes=64)
         sg = sb.tile([P, G, N], F32, name="sg", align_bytes=64)
         y = sb.tile([P, G, N], F32, name="y", align_bytes=64)
         warm_in = sb.tile([P, 8], F32, name="warm_in")
         warm_out = sb.tile([P, 8], F32, name="warm_out")
-        z_bank = [ps.tile([P, N], F32, name="z_bank%d" % g) for g in range(G)]
-        g_bank = [ps.tile([P, N], F32, name="g_bank%d" % g) for g in range(G)]
+        bank_p = [ps.tile([P, N], F32, name="bank_p%d" % g) for g in range(G)]
+        bank_q = [ps.tile([P, N], F32, name="bank_q%d" % g) for g in range(G)]
 
         x_rows = x.rearrange("g (p j) l -> (g p) j l", j=PACK)
 
@@ -60,25 +60,26 @@ def tile_rows_conv_wave_kernel(tc, x, w0, w1, u0, u1, out):
                 in_=src.rearrange("p j (c r) -> p c j r", r=RUN),
             )
 
-        def copy_x(l0, l1):
-            interleave(nc.vector.tensor_copy, x_bf[:, PACK * l0 : PACK * l1], x_raw[:, :, l0:l1])
+        def copy_x(l0, l1, engine_copy=nc.vector.tensor_copy):
+            interleave(engine_copy, x_bf[:, PACK * l0 : PACK * l1], x_raw[:, :, l0:l1])
 
-        def copy_w(engine_copy, i):
-            interleave(engine_copy, w_bf[:, i, :], w_raw[:, i, :, :])
+        def copy_w(engine_copy, i, m0=0, m1=M):
+            interleave(engine_copy, w_bf[:, i, PACK * m0 : PACK * m1], w_raw[:, i, :, m0:m1])
 
         def quantize_x(l0, l1):
             nc.vector.quantize_mx(
-                out=x_codes[:, HALF + l0 : HALF + l1].bitcast(FP8X4),
-                scales=x_scales[:, HALF + l0 : HALF + l1],
+                out=x_codes[:, PAD + l0 : PAD + l1].bitcast(FP8X4),
+                scales=x_scales[:, PAD + l0 : PAD + l1],
                 in_=x_bf[:, PACK * l0 : PACK * l1],
             )
 
         def quantize_w(i):
             nc.vector.quantize_mx(out=w_codes[:, i, :].bitcast(FP8X4), scales=w_scales[:, i, :], in_=w_bf[:, i, :])
 
-        def tap(banks, g, i, half, shift):
+        def tap(banks, g, i, end, shift):
             rows = slice(g * ROWS, (g + 1) * ROWS)
-            cols = slice(half * HALF + shift * DIL, half * HALF + shift * DIL + N)
+            stop = PAD + end + shift * DIL
+            cols = slice(stop - N, stop)
             nc.tensor.matmul_mx(
                 out=banks[g][:],
                 lhsT=w_codes[rows, i, :].bitcast(FP8X4),
@@ -89,17 +90,26 @@ def tile_rows_conv_wave_kernel(tc, x, w0, w1, u0, u1, out):
                 stop=(shift == 1),
             )
 
-        def taps(banks, i, half, shift):
+        def taps(banks, i, end, shift):
             for g in range(G):
-                tap(banks, g, i, half, shift)
+                tap(banks, g, i, end, shift)
 
-        def act(func, dst, banks, g, half):
-            nc.scalar.activation(out=dst[:, g, half * HALF : (half + 1) * HALF], in_=banks[g][:, HALF:], func=func)
+        def act(func, dst, banks, g, n0, n1, end):
+            nc.scalar.activation(out=dst[:, g, n0:n1], in_=banks[g][:, N - end + n0 : N - end + n1], func=func)
 
-        def finish(g, half):
-            cols = slice(half * HALF, (half + 1) * HALF)
-            nc.vector.tensor_tensor(out=y[:, g, cols], in0=th[:, g, cols], in1=sg[:, g, cols], op=ALU.mult)
-            nc.sync.dma_start(out=out[g, :, cols], in_=y[:, g, cols])
+        def acts(func, dst, banks, n0, n1):
+            for g in range(G):
+                act(func, dst, banks, g, n0, n1, n1)
+
+        def mult(g, n0, n1):
+            nc.vector.tensor_tensor(out=y[:, g, n0:n1], in0=th[:, g, n0:n1], in1=sg[:, g, n0:n1], op=ALU.mult)
+
+        def store(g, n0, n1):
+            nc.sync.dma_start(out=out[g, :, n0:n1], in_=y[:, g, n0:n1])
+
+        def finish(g, n0, n1):
+            mult(g, n0, n1)
+            store(g, n0, n1)
 
         load_x(0, 256)
         load_w(W0, w0)
@@ -111,49 +121,54 @@ def tile_rows_conv_wave_kernel(tc, x, w0, w1, u0, u1, out):
         load_x(512, 640)
 
         nc.gpsimd.memset(warm_in[:], 0.0)
-        nc.gpsimd.memset(x_codes[:, :HALF], 0)
-        nc.gpsimd.memset(x_scales[:, :HALF].bitcast(U32), 0)
+        nc.gpsimd.memset(x_codes[:, :PAD], 0)
+        nc.gpsimd.memset(x_scales[:, :PAD].bitcast(U32), 0)
         nc.scalar.activation(out=warm_out[:], in_=warm_in[:], func=ACT.Sigmoid)
 
         copy_x(0, 256)
+        copy_w(nc.vector.tensor_copy, W0)
         quantize_x(0, 256)
-        copy_w(nc.scalar.copy, W0)
         quantize_w(W0)
-        taps(z_bank, W0, 0, 0)
+        taps(bank_p, W0, 256, 0)
         copy_w(nc.scalar.copy, W1)
         copy_x(256, 384)
         quantize_w(W1)
         quantize_x(256, 384)
-        taps(z_bank, W1, 0, 1)
-        for g in range(G):
-            act(ACT.Tanh, th, z_bank, g, 0)
-
+        taps(bank_p, W1, 256, 1)
+        copy_w(nc.scalar.copy, U1, 64, 128)
+        acts(ACT.Tanh, th, bank_p, 0, 256)
         copy_w(nc.vector.tensor_copy, U0)
+        copy_w(nc.vector.tensor_copy, U1, 0, 64)
         quantize_w(U0)
-        taps(g_bank, U0, 0, 0)
-        copy_w(nc.vector.tensor_copy, U1)
+        taps(bank_q, U0, 256, 0)
         quantize_w(U1)
-        taps(g_bank, U1, 0, 1)
-        for g in range(G):
-            act(ACT.Sigmoid, sg, g_bank, g, 0)
-
+        taps(bank_q, U1, 256, 1)
+        acts(ACT.Sigmoid, sg, bank_q, 0, 256)
         copy_x(384, 512)
         quantize_x(384, 512)
-        taps(z_bank, W0, 1, 0)
+        taps(bank_p, W0, 512, 0)
         copy_x(512, 640)
         quantize_x(512, 640)
-        taps(z_bank, W1, 1, 1)
-        tap(g_bank, 0, U0, 1, 0)
+        taps(bank_p, W1, 512, 1)
+        tap(bank_q, 0, U0, 512, 0)
         for g in range(G):
             if g + 1 < G:
-                tap(g_bank, g + 1, U0, 1, 0)
-            tap(g_bank, g, U1, 1, 1)
+                tap(bank_q, g + 1, U0, 512, 0)
+            tap(bank_q, g, U1, 512, 1)
         for g in range(G):
-            finish(g, 0)
-
-        act(ACT.Tanh, th, z_bank, 0, 1)
-        for g in range(G):
-            if g + 1 < G:
-                act(ACT.Tanh, th, z_bank, g + 1, 1)
-            act(ACT.Sigmoid, sg, g_bank, g, 1)
-            finish(g, 1)
+            finish(g, 0, 256)
+        act(ACT.Tanh, th, bank_p, 0, 256, 512, 512)
+        act(ACT.Tanh, th, bank_p, 1, 256, 512, 512)
+        act(ACT.Sigmoid, sg, bank_q, 0, 256, 512, 512)
+        finish(0, 256, 512)
+        act(ACT.Sigmoid, sg, bank_q, 1, 256, 512, 512)
+        finish(1, 256, 512)
+        act(ACT.Tanh, th, bank_p, 2, 256, 512, 512)
+        act(ACT.Sigmoid, sg, bank_q, 2, 256, 512, 512)
+        finish(2, 256, 512)
+        act(ACT.Tanh, th, bank_p, 3, 256, 512, 512)
+        act(ACT.Sigmoid, sg, bank_q, 3, 256, 384, 512)
+        mult(3, 256, 384)
+        act(ACT.Sigmoid, sg, bank_q, 3, 384, 512, 512)
+        mult(3, 384, 512)
+        store(3, 256, 512)

@@ -124,37 +124,40 @@ def tile_rows_conv_wave_kernel(tc, x, w0, w1, u0, u1, out):
         nc.gpsimd.memset(x_codes[:, :PAD], 0)
         nc.gpsimd.memset(x_scales[:, :PAD].bitcast(U32), 0)
         nc.scalar.activation(out=warm_out[:], in_=warm_in[:], func=ACT.Sigmoid)
-
+        V, S = nc.vector.tensor_copy, nc.scalar.copy
         copy_x(0, 256)
-        copy_w(nc.vector.tensor_copy, W0)
+        copy_w(V, W0)
         quantize_x(0, 256)
         quantize_w(W0)
-        taps(bank_p, W0, 256, 0)
-        copy_w(nc.scalar.copy, W1)
-        copy_x(256, 384)
+        for g in (1, 2, 3, 0):
+            tap(bank_p, g, W0, 256, 0)
+        copy_w(S, W1, 64, 128)
+        copy_w(V, W1, 0, 64)
+        copy_x(256, 320)
+        copy_x(320, 352)
+        copy_x(352, 384, S)
         quantize_w(W1)
-        quantize_x(256, 384)
+        quantize_x(256, 320)
+        quantize_x(320, 384)
         taps(bank_p, W1, 256, 1)
-        copy_w(nc.scalar.copy, U1, 64, 128)
+        copy_w(S, U0, 80, 128)
+        copy_w(S, U1, 64, 128)
         acts(ACT.Tanh, th, bank_p, 0, 256)
-        copy_w(nc.vector.tensor_copy, U0)
-        copy_w(nc.vector.tensor_copy, U1, 0, 64)
+        copy_w(V, U0, 0, 80)
         quantize_w(U0)
         taps(bank_q, U0, 256, 0)
+        copy_w(V, U1, 0, 64)
         quantize_w(U1)
         taps(bank_q, U1, 256, 1)
         acts(ACT.Sigmoid, sg, bank_q, 0, 256)
         copy_x(384, 512)
+        copy_x(512, 640)
         quantize_x(384, 512)
         taps(bank_p, W0, 512, 0)
-        copy_x(512, 640)
         quantize_x(512, 640)
         taps(bank_p, W1, 512, 1)
-        tap(bank_q, 0, U0, 512, 0)
-        for g in range(G):
-            if g + 1 < G:
-                tap(bank_q, g + 1, U0, 512, 0)
-            tap(bank_q, g, U1, 512, 1)
+        for g, i in [(0,0),(1,0),(0,1),(2,0),(1,1),(3,0),(2,1),(3,1)]:
+            tap(bank_q, g, (U0, U1)[i], 512, i)
         for g in range(G):
             finish(g, 0, 256)
         act(ACT.Tanh, th, bank_p, 0, 256, 512, 512)

@@ -90,6 +90,18 @@ def tile_rows_conv_wave_kernel(tc, x, w0, w1, u0, u1, out):
                 stop=(shift == 1),
             )
 
+        def warm_pass(g):
+            rows = slice(g * ROWS, (g + 1) * ROWS)
+            nc.tensor.matmul_mx(
+                out=bank_q[g][:],
+                lhsT=w_codes[rows, W0, :].bitcast(FP8X4),
+                lhsT_scale=w_scales[rows, W0, :],
+                rhs=x_codes[rows, 0:N].bitcast(FP8X4),
+                rhs_scale=x_scales[rows, 0:N],
+                start=True,
+                stop=True,
+            )
+
         def taps(banks, i, end, shift):
             for g in range(G):
                 tap(banks, g, i, end, shift)
@@ -131,6 +143,8 @@ def tile_rows_conv_wave_kernel(tc, x, w0, w1, u0, u1, out):
         quantize_w(W0)
         for g in (1, 2, 3, 0):
             tap(bank_p, g, W0, 256, 0)
+        for g in (1, 2, 3):
+            warm_pass(g)
         copy_w(S, W1, 64, 128)
         copy_w(V, W1, 0, 64)
         copy_x(256, 320)

from contextlib import ExitStack

import concourse.mybir as mybir

G, D, M, N, L = 4, 128, 128, 512, 640
FLOPS = 2 * 4 * G * D * M * N

F32 = mybir.dt.float32
BF16 = mybir.dt.bfloat16
U32 = mybir.dt.uint32
U8 = mybir.dt.uint8
FP8X4 = mybir.dt.float8_e4m3fn_x4
ACT = mybir.ActivationFunctionType
ALU = mybir.AluOpType

P = 128
PACK = 4
ROWS = D // PACK
DIL = 128
PAD = 256
RUN = 4
W0, W1, U0, U1 = range(4)


def tile_rows_conv_wave_kernel(tc, x, w0, w1, u0, u1, out):
    nc = tc.nc

    with ExitStack() as ctx:
        sb = ctx.enter_context(tc.tile_pool(name="sb", bufs=1))
        ps = ctx.enter_context(tc.psum_pool(name="ps", bufs=1))
        ctx.enter_context(tc.manual_schedule())

        w_raw = sb.tile([P, 4, PACK, M], F32, name="w_raw", align_bytes=64)
        w_bf = sb.tile([P, 4, M * PACK], BF16, name="w_bf", align_bytes=64)
        w_codes = sb.tile([P, 4, M], U32, name="w_codes", align_bytes=64)
        w_scales = sb.tile([P, 4, M], U8, name="w_scales", align_bytes=64)
        x_raw = sb.tile([P, PACK, L], F32, name="x_raw", align_bytes=64)
        x_bf = sb.tile([P, L * PACK], BF16, name="x_bf", align_bytes=64)
        x_codes = sb.tile([P, PAD + L], U32, name="x_codes", align_bytes=64)
        x_scales = sb.tile([P, PAD + L], U8, name="x_scales", align_bytes=64)
        th = sb.tile([P, G, N], F32, name="th", align_bytes=64)
        sg = sb.tile([P, G, N], F32, name="sg", align_bytes=64)
        y = sb.tile([P, G, N], F32, name="y", align_bytes=64)
        warm_in = sb.tile([P, 8], F32, name="warm_in")
        warm_out = sb.tile([P, 8], F32, name="warm_out")
        bank_p = [ps.tile([P, N], F32, name="bank_p%d" % g) for g in range(G)]
        bank_q = [ps.tile([P, N], F32, name="bank_q%d" % g) for g in range(G)]

        x_rows = x.rearrange("g (p j) l -> (g p) j l", j=PACK)

        def load_x(l0, l1):
            nc.sync.dma_start(out=x_raw[:, :, l0:l1], in_=x_rows[:, :, l0:l1])

        def load_w(i, w):
            nc.sync.dma_start(out=w_raw[:, i, :, :], in_=w.rearrange("g (p j) m -> (g p) j m", j=PACK))

        def interleave(engine_copy, dst, src):
            engine_copy(
                out=dst.rearrange("p (c r j) -> p c j r", r=RUN, j=PACK),
                in_=src.rearrange("p j (c r) -> p c j r", r=RUN),
            )

        def copy_x(l0, l1, engine_copy=nc.vector.tensor_copy):
            interleave(engine_copy, x_bf[:, PACK * l0 : PACK * l1], x_raw[:, :, l0:l1])

        def copy_w(engine_copy, i, m0=0, m1=M):
            interleave(engine_copy, w_bf[:, i, PACK * m0 : PACK * m1], w_raw[:, i, :, m0:m1])

        def quantize_x(l0, l1):
            nc.vector.quantize_mx(
                out=x_codes[:, PAD + l0 : PAD + l1].bitcast(FP8X4),
                scales=x_scales[:, PAD + l0 : PAD + l1],
                in_=x_bf[:, PACK * l0 : PACK * l1],
            )

        def quantize_w(i):
            nc.vector.quantize_mx(out=w_codes[:, i, :].bitcast(FP8X4), scales=w_scales[:, i, :], in_=w_bf[:, i, :])

        def tap(banks, g, i, end, shift):
            rows = slice(g * ROWS, (g + 1) * ROWS)
            stop = PAD + end + shift * DIL
            cols = slice(stop - N, stop)
            nc.tensor.matmul_mx(
                out=banks[g][:],
                lhsT=w_codes[rows, i, :].bitcast(FP8X4),
                lhsT_scale=w_scales[rows, i, :],
                rhs=x_codes[rows, cols].bitcast(FP8X4),
                rhs_scale=x_scales[rows, cols],
                start=(shift == 0),
                stop=(shift == 1),
            )

        def warm_pass(g):
            rows = slice(g * ROWS, (g + 1) * ROWS)
            nc.tensor.matmul_mx(
                out=bank_q[g][:],
                lhsT=w_codes[rows, W0, :].bitcast(FP8X4),
                lhsT_scale=w_scales[rows, W0, :],
                rhs=x_codes[rows, 0:N].bitcast(FP8X4),
                rhs_scale=x_scales[rows, 0:N],
                start=True,
                stop=True,
            )

        def taps(banks, i, end, shift):
            for g in range(G):
                tap(banks, g, i, end, shift)

        def act(func, dst, banks, g, n0, n1, end):
            nc.scalar.activation(out=dst[:, g, n0:n1], in_=banks[g][:, N - end + n0 : N - end + n1], func=func)

        def acts(func, dst, banks, n0, n1):
            for g in range(G):
                act(func, dst, banks, g, n0, n1, n1)

        def mult(g, n0, n1):
            nc.vector.tensor_tensor(out=y[:, g, n0:n1], in0=th[:, g, n0:n1], in1=sg[:, g, n0:n1], op=ALU.mult)

        def store(g, n0, n1):
            nc.sync.dma_start(out=out[g, :, n0:n1], in_=y[:, g, n0:n1])

        def finish(g, n0, n1):
            mult(g, n0, n1)
            store(g, n0, n1)

        load_x(0, 256)
        load_w(W0, w0)
        load_w(W1, w1)
        load_x(256, 384)
        load_w(U0, u0)
        load_w(U1, u1)
        load_x(384, 512)
        load_x(512, 640)

        nc.gpsimd.memset(warm_in[:], 0.0)
        nc.gpsimd.memset(x_codes[:, :PAD], 0)
        nc.gpsimd.memset(x_scales[:, :PAD].bitcast(U32), 0)
        nc.scalar.activation(out=warm_out[:], in_=warm_in[:], func=ACT.Sigmoid)
        V, S = nc.vector.tensor_copy, nc.scalar.copy
        copy_x(0, 256)
        copy_w(V, W0)
        quantize_x(0, 256)
        quantize_w(W0)
        for g in (1, 2, 3, 0):
            tap(bank_p, g, W0, 256, 0)
        for g in (1, 2, 3):
            warm_pass(g)
        copy_w(S, W1, 64, 128)
        copy_w(V, W1, 0, 64)
        copy_x(256, 320)
        copy_x(320, 352)
        copy_x(352, 384, S)
        quantize_w(W1)
        quantize_x(256, 320)
        quantize_x(320, 384)
        taps(bank_p, W1, 256, 1)
        copy_w(S, U0, 80, 128)
        copy_w(S, U1, 64, 128)
        acts(ACT.Tanh, th, bank_p, 0, 256)
        copy_w(V, U0, 0, 80)
        quantize_w(U0)
        taps(bank_q, U0, 256, 0)
        copy_w(V, U1, 0, 64)
        quantize_w(U1)
        taps(bank_q, U1, 256, 1)
        acts(ACT.Sigmoid, sg, bank_q, 0, 256)
        copy_x(384, 512)
        copy_x(512, 640)
        quantize_x(384, 512)
        taps(bank_p, W0, 512, 0)
        quantize_x(512, 640)
        taps(bank_p, W1, 512, 1)
        for g, i in [(0,0),(1,0),(0,1),(2,0),(1,1),(3,0),(2,1),(3,1)]:
            tap(bank_q, g, (U0, U1)[i], 512, i)
        for g in range(G):
            finish(g, 0, 256)
        act(ACT.Tanh, th, bank_p, 0, 256, 512, 512)
        act(ACT.Tanh, th, bank_p, 1, 256, 512, 512)
        act(ACT.Sigmoid, sg, bank_q, 0, 256, 512, 512)
        finish(0, 256, 512)
        act(ACT.Sigmoid, sg, bank_q, 1, 256, 512, 512)
        finish(1, 256, 512)
        act(ACT.Tanh, th, bank_p, 2, 256, 512, 512)
        act(ACT.Sigmoid, sg, bank_q, 2, 256, 512, 512)
        finish(2, 256, 512)
        act(ACT.Tanh, th, bank_p, 3, 256, 512, 512)
        act(ACT.Sigmoid, sg, bank_q, 3, 256, 384, 512)
        mult(3, 256, 384)
        act(ACT.Sigmoid, sg, bank_q, 3, 384, 512, 512)
        mult(3, 384, 512)
        store(3, 256, 512)
